import numpy as np
import ml_dtypes


def mxq(x, axis, fmt="e4m3"):
    dtype, down = {"e4m3": (ml_dtypes.float8_e4m3fn, 7), "e5m2": (ml_dtypes.float8_e5m2, 14)}[fmt]
    v = np.moveaxis(np.asarray(x, np.float32).astype(ml_dtypes.bfloat16).astype(np.float64), axis, -1)
    blocks = v.reshape(v.shape[:-1] + (-1, 32))
    amax = np.abs(blocks).max(-1, keepdims=True)
    byte = np.maximum(np.where(amax > 0, np.frexp(amax)[1] - 1 + 127, 0) - down, 1)
    scale = np.exp2(byte - 127.0)
    codes = (blocks / scale).astype(np.float32).astype(dtype).astype(np.float64)
    return np.moveaxis((codes * scale).reshape(v.shape), -1, axis)


WIDE = False


def mx_kscale(k):
    if not WIDE:
        return np.ones(k)
    levels = np.array([10, -10, 5, -5, 0])
    if k % 512:
        return np.exp2(np.random.permutation(np.resize(levels, k // 32))).repeat(32)
    a = np.empty((k // 512, 16))
    for p in range(k // 512):
        a[p, :8] = np.random.permutation(np.resize(levels, 8))
        for g in range(8):
            far = levels[np.abs(levels - a[p, g]) >= 10]
            a[p, g + 8] = far[np.random.randint(len(far))]
    return np.exp2(a.ravel()).repeat(32)


def f64(x):
    return np.asarray(x).astype(np.float64)


def striped(idx):
    return np.tile(idx.reshape(-1, 16).T, (8, 1)).astype(np.uint16)


def unstriped(offs):
    return offs[:16].T.reshape(-1).astype(np.int64)


E2M1 = np.array([0.0, 0.5, 1.0, 1.5, 2.0, 3.0, 4.0, 6.0, -0.0, -0.5, -1.0, -1.5, -2.0, -3.0, -4.0, -6.0])


def pack_weight(w, fmt):
    k, n = w.shape
    w = f64(np.asarray(w, np.float32).astype(ml_dtypes.bfloat16)).reshape(k // 32, 32, n)
    amax = np.abs(w).max(1)
    if fmt == "e4m3":
        byte = np.frexp(amax)[1] - 1 + 127 - 7
    else:
        mant, ex = np.frexp(amax / 6.0)
        byte = np.where(mant > 0.5, ex, ex - 1) + 127
    byte = np.clip(np.where(amax > 0, byte, 1), 1, 254)
    scaled = (w * np.exp2(127.0 - byte)[:, None, :]).reshape(k, n).astype(np.float32)
    by_word = np.ascontiguousarray(scaled.reshape(k // 512, 128, 4, n).transpose(0, 1, 3, 2))
    if fmt == "e4m3":
        words = by_word.astype(ml_dtypes.float8_e4m3fn).view(np.uint8)
    else:
        c = by_word.astype(ml_dtypes.float4_e2m1fn).view(np.uint8) & 0xF
        words = (c[..., 0::2] | (c[..., 1::2] << 4)).reshape(k // 512, 128, 2 * n)
    return np.ascontiguousarray(words), np.ascontiguousarray(byte.astype(np.uint8).reshape(k // 512, 16, n))


def unpack_weight(words, scales, fmt):
    g, _, n = scales.shape
    words = np.ascontiguousarray(words).reshape(g, 128, n, -1)
    if fmt == "e4m3":
        vals = words.view(ml_dtypes.float8_e4m3fn).astype(np.float64)
    else:
        nib = np.empty((g, 128, n, 4), np.uint8)
        nib[..., 0::2] = words & 0xF
        nib[..., 1::2] = words >> 4
        vals = E2M1[nib]
    vals = vals * np.repeat(np.exp2(scales.astype(np.float64) - 127.0), 8, axis=1)[..., None]
    return vals.transpose(0, 1, 3, 2).reshape(g * 512, n)


def gelu(v):
    return 0.5 * v * (1.0 + np.tanh(np.sqrt(2.0 / np.pi) * (v + 0.044715 * v**3)))


K, T, S, S2 = 1024, 2048, 512, 1024

def setup_inputs():
    n = np.random.standard_normal
    s = mx_kscale(K)[:, None]
    d = {}
    d["tab_words"], d["tab_scales"] = pack_weight(n((K, T)) * s, "e4m3")
    d["offs"] = striped(np.random.permutation(T)[:S])
    d["offs2"] = striped(np.random.permutation(T)[:S2])
    d["w1"] = (1.3 * n((K, K)) / s / s.T / K).astype(np.float32)
    d["w2_words"], d["w2_scales"] = pack_weight(n((K, K)) * s / s.T / K**0.5, "e2m1")
    d["prior"] = (0.8 * n((S2, S))).astype(np.float32)
    return d

def reference(tab_words, tab_scales, offs, offs2, w1, w2_words, w2_scales, prior):
    TW = unpack_weight(tab_words, tab_scales, "e4m3")
    v = TW[:, unstriped(offs)]
    v2 = TW[:, unstriped(offs2)]
    w2 = unpack_weight(w2_words, w2_scales, "e2m1")
    a = mxq(f64(w1), 0, "e4m3").T @ v
    b = w2.T @ mxq(np.abs(a), 0, "e4m3")
    h = np.maximum(a, b)
    e = v2.T @ mxq(h, 0, "e4m3")
    x = e + f64(prior)
    return 0.5 * x * (1.0 + np.tanh(0.7978845608028654 * (x + 0.044715 * x**3)))

@@ -1,0 +1,249 @@
+from contextlib import ExitStack
+
+import concourse.mybir as mybir
+
+K, T, S, S2 = 1024, 2048, 512, 1024
+FLOPS = 2 * K * K * S * 2 + 2 * K * S2 * S
+
+F32 = mybir.dt.float32
+BF16 = mybir.dt.bfloat16
+I32 = mybir.dt.int32
+U32 = mybir.dt.uint32
+U16 = mybir.dt.uint16
+U8 = mybir.dt.uint8
+FP8X4 = mybir.dt.float8_e4m3fn_x4
+FP4X4 = mybir.dt.float4_e2m1fn_x4
+ACT = mybir.ActivationFunctionType
+ALU = mybir.AluOpType
+
+P = 128
+PACK = 4
+K_PASS = P * PACK
+PASSES = K // K_PASS
+CHUNK = 128
+CHUNKS = S // CHUNK
+QUADRANTS = 4
+ROWS = 4
+
+
+def tile_list_lens_pair_balance_kernel(
+    tc, tab_words, tab_scales, offs, offs2, w1, w2_words, w2_scales, prior, out
+):
+    nc = tc.nc
+    with ExitStack() as ctx:
+        keep = ctx.enter_context(tc.tile_pool(name="keep", bufs=1))
+        psum = ctx.enter_context(tc.psum_pool(name="psum", bufs=8))
+
+        def sbuf(name, shape, dtype, tag=None):
+            return keep.tile(shape, dtype, name=name, tag=tag or name, align_bytes=64)
+
+        def new_bank():
+            return psum.tile([P, PACK, CHUNK], F32, name="bank")
+
+        rear_list = sbuf("rear_list", [P, S // 16], U16)
+        front_list = sbuf("front_list", [P, S2 // 16], U16)
+        tab_plane = sbuf("tab_plane", [P, T], U8)
+        w2_plane_raw = sbuf("w2_plane_raw", [P, PASSES * K], U8)
+        nc.gpsimd.memset(tab_plane[:].bitcast(I32), 0)
+        nc.gpsimd.memset(w2_plane_raw[:].bitcast(I32), 0)
+        warm_in = sbuf("warm_in", [P, 8], F32)
+        warm_out = sbuf("warm_out", [P, 8], F32)
+        nc.gpsimd.memset(warm_in[:], 0.0)
+        nc.scalar.activation(warm_out[:], warm_in[:], ACT.Gelu_apprx_tanh)
+
+        tab = [sbuf("tab%d" % a, [P, T], I32) for a in range(PASSES)]
+        w1_raw = {}
+
+        def load_tab(a):
+            nc.sync.dma_start(tab[a][:], tab_words[a].rearrange("p n i -> p (n i)").bitcast(I32))
+
+        def load_w1(a, b, pieces=1):
+            width = K_PASS // pieces
+            w1_raw[a, b] = []
+            for h in range(pieces):
+                raw = sbuf("w1_raw%d%d%d" % (a, b, h), [P, PACK, width], F32)
+                c0 = K_PASS * b + width * h
+                rows = w1[K_PASS * a : K_PASS * (a + 1), c0 : c0 + width]
+                nc.sync.dma_start(raw[:], rows.rearrange("(p i) c -> p i c", i=PACK))
+                w1_raw[a, b].append(raw)
+
+        nc.sync.dma_start(rear_list[:], offs)
+        nc.sync.dma_start(front_list[:], offs2)
+        w2_raw = sbuf("w2_raw", [P, PASSES, K // 2], I32)
+        nc.sync.dma_start(w2_raw[:], w2_words.rearrange("a p n -> p a n").bitcast(I32))
+        for q in range(QUADRANTS):
+            nc.sync.dma_start(
+                tab_plane[32 * q : 32 * q + PASSES * ROWS, :].bitcast(I32),
+                tab_scales[:, ROWS * q : ROWS * (q + 1), :].bitcast(I32),
+            )
+        load_w1(0, 0)
+        load_w1(1, 0)
+        for q in range(QUADRANTS):
+            nc.sync.dma_start(
+                w2_plane_raw[32 * q : 32 * q + ROWS, :].bitcast(I32).rearrange("r (a n) -> r a n", a=PASSES),
+                w2_scales[:, ROWS * q : ROWS * (q + 1), :].bitcast(I32).rearrange("a r n -> r a n"),
+            )
+        load_tab(0)
+        load_w1(0, 1)
+        load_tab(1)
+        load_w1(1, 1, pieces=2)
+        prior_sb = []
+        for g in range(2):
+            prior_sb.append(sbuf("prior%d" % g, [P, PACK, S], F32))
+            nc.sync.dma_start(
+                prior_sb[g][:], prior[K_PASS * g : K_PASS * (g + 1), :].rearrange("(u p) j -> p u j", p=P)
+            )
+
+        def gather(name, window, offsets, count, dtype, piece, tag=None):
+            picked = sbuf(name, [P, count], dtype, tag)
+            for j0 in range(0, count, piece):
+                nc.vector.tensor_copy(
+                    picked[:, j0 : j0 + piece], window.indirect(offsets[:, j0 // 16 : (j0 + piece) // 16])
+                )
+            return picked
+
+        def quantize(name, values, width, piece):
+            codes = sbuf(name + "_codes", [P, width], U32)
+            plane = sbuf(name + "_plane", [P, width], U8)
+            for c0 in range(0, width, piece):
+                nc.vector.quantize_mx(
+                    out=codes[:, c0 : c0 + piece].bitcast(FP8X4),
+                    scales=plane[:, c0 : c0 + piece],
+                    in_=values[:, PACK * c0 : PACK * (c0 + piece)],
+                )
+            return codes, plane
+
+        def quantize_w1(a, b, vector_share, piece):
+            dealt = sbuf("w1_dealt%d%d" % (a, b), [P, PACK * K_PASS], BF16)
+            dst = dealt[:].rearrange("p (t m i) -> p m i t", t=PACK, i=PACK)
+            m0 = 0
+            for raw in w1_raw[a, b]:
+                src = raw[:].rearrange("p i (m t) -> p m i t", t=PACK)
+                count = src.shape[1]
+                split = count - (vector_share if raw is w1_raw[a, b][-1] else 0)
+                nc.scalar.copy(dst[:, m0 : m0 + split], src[:, :split])
+                if split < count:
+                    nc.vector.tensor_copy(dst[:, m0 + split : m0 + count], src[:, split:])
+                m0 = m0 + count
+            return quantize("w1_%d%d" % (a, b), dealt, K_PASS, piece)
+
+        def mx_pass(bank, a, stationary, moving):
+            for t in range(PACK):
+                nc.tensor.matmul_mx(
+                    out=bank[:, t, :],
+                    lhsT=stationary(t)[0],
+                    lhsT_scale=stationary(t)[1],
+                    rhs=moving[0],
+                    rhs_scale=moving[1],
+                    start=(a == 0 and t == 0),
+                    stop=(a == PASSES - 1 and t == PACK - 1),
+                )
+
+        def interleaved(bank):
+            return bank[:].rearrange("p t j -> p j t")
+
+        def cols(i):
+            return slice(P * i, P * (i + 1))
+
+        rear_plane = gather("rear_plane", tab_plane[:], rear_list, S, U8, S)
+        w1_q = {}
+        w1_q[0, 0] = quantize_w1(0, 0, 0, K_PASS)
+        w1_q[1, 0] = quantize_w1(1, 0, 0, K_PASS)
+        rear = [gather("rear0", tab[0][:].bitcast(U32), rear_list, S, U32, S)]
+        a_bank = {}
+
+        def stage1_pass(a, b, c):
+            codes, plane = w1_q[a, b]
+            mx_pass(
+                a_bank[b, c],
+                a,
+                lambda t: (codes[:, cols(t)].bitcast(FP8X4), plane[:, cols(t)]),
+                (rear[a][:, cols(c)].bitcast(FP8X4), rear_plane[ROWS * a :, cols(c)]),
+            )
+
+        for c in range(CHUNKS):
+            a_bank[0, c] = new_bank()
+            stage1_pass(0, 0, c)
+        w1_q[0, 1] = quantize_w1(0, 1, 0, K_PASS)
+        for c in range(CHUNKS):
+            a_bank[1, c] = new_bank()
+            stage1_pass(0, 1, c)
+        rear.append(gather("rear1", tab[1][:].bitcast(U32), rear_list, S, U32, S // 2))
+        w1_q[1, 1] = quantize_w1(1, 1, 32, 2 * P)
+
+        w2_codes = sbuf("w2_codes", [P, PASSES * 2 * K], U8)
+        w2_plane = sbuf("w2_plane", [P, PASSES * K], U8)
+
+        def deal_w2():
+            nc.vector.tensor_copy(
+                w2_plane[:].rearrange("p (g t m) -> p g t m", t=PACK, m=P),
+                w2_plane_raw[:].rearrange("p (g m t) -> p g t m", t=PACK, m=P),
+            )
+            for a in range(PASSES):
+                nc.vector.tensor_copy(
+                    w2_codes[:, 2 * K * a : 2 * K * (a + 1)].bitcast(U16).rearrange("p (b t m) -> p b t m", t=PACK, m=P),
+                    w2_raw[:, a, :].bitcast(U16).rearrange("p (b m t) -> p b t m", t=PACK, m=P),
+                )
+
+        front = []
+        front_plane = []
+
+        def gather_front():
+            front_plane.append(gather("front_plane", tab_plane[:], front_list, S2, U8, S2))
+            front.append(gather("front0", tab[0][:].bitcast(U32), front_list, S2, U32, S2))
+            front.append(gather("front1", tab[1][:].bitcast(U32), front_list, S2, U32, S, tag="w1_dealt11"))
+
+        for c in range(CHUNKS):
+            abs_q, a_kept = [], []
+            for b in range(PASSES):
+                stage1_pass(1, b, c)
+                abs_a = sbuf("abs_a%d%d" % (b, c), [P, PACK * CHUNK], BF16)
+                nc.scalar.activation(
+                    abs_a[:].rearrange("p (j t) -> p j t", t=PACK), interleaved(a_bank[b, c]), ACT.Abs
+                )
+                abs_q.append(quantize("abs_a%d%d" % (b, c), abs_a, CHUNK, CHUNK))
+            for b in range(PASSES):
+                a_kept.append(sbuf("a_kept%d%d" % (b, c), [P, CHUNK, PACK], F32))
+                nc.scalar.copy(a_kept[b][:], interleaved(a_bank[b, c]))
+            if c == 0:
+                deal_w2()
+            h_values = []
+            for b in range(PASSES):
+                b_bank = new_bank()
+                for a in range(PASSES):
+                    base = K * a + K_PASS * b
+                    mx_pass(
+                        b_bank,
+                        a,
+                        lambda t: (
+                            w2_codes[:, 2 * (base + P * t) : 2 * (base + P * (t + 1))].bitcast(FP4X4),
+                            w2_plane[:, base + P * t : base + P * (t + 1)],
+                        ),
+                        (abs_q[a][0][:].bitcast(FP8X4), abs_q[a][1][:]),
+                    )
+                h_values.append(sbuf("h%d%d" % (b, c), [P, PACK * CHUNK], BF16))
+                nc.vector.tensor_tensor(
+                    h_values[b][:].rearrange("p (j t) -> p j t", t=PACK), interleaved(b_bank), a_kept[b][:], ALU.max
+                )
+            h_q = [quantize("h%d%d" % (b, c), h_values[b], CHUNK, CHUNK) for b in range(PASSES)]
+            if c == 0:
+                gather_front()
+            for g in range(2):
+                e_bank = new_bank()
+                for a in range(PASSES):
+                    mx_pass(
+                        e_bank,
+                        a,
+                        lambda u: (
+                            front[a][:, cols(PACK * g + u)].bitcast(FP8X4),
+                            front_plane[0][ROWS * a :, cols(PACK * g + u)],
+                        ),
+                        (h_q[a][0][:].bitcast(FP8X4), h_q[a][1][:]),
+                    )
+                x = sbuf("x%d%d" % (g, c), [P, PACK, CHUNK], F32)
+                nc.vector.tensor_tensor(x[:], e_bank[:], prior_sb[g][:, :, cols(c)], ALU.add)
+                y = sbuf("y%d%d" % (g, c), [P, PACK, CHUNK], F32)
+                nc.scalar.activation(y[:], x[:], ACT.Gelu_apprx_tanh)
+                nc.sync.dma_start(
+                    out[K_PASS * g : K_PASS * (g + 1), cols(c)].rearrange("(u p) j -> p u j", p=P), y[:]
+                )

@@ -32,10 +32,18 @@ def tile_list_lens_pair_balance_kernel(
     nc = tc.nc
     with ExitStack() as ctx:
         keep = ctx.enter_context(tc.tile_pool(name="keep", bufs=1))
+        shared = ctx.enter_context(tc.tile_pool(name="shared", bufs=1))
         psum = ctx.enter_context(tc.psum_pool(name="psum", bufs=8))
 
         def sbuf(name, shape, dtype, tag=None):
             return keep.tile(shape, dtype, name=name, tag=tag or name, align_bytes=64)
+
+        places = {"a_kept01": 0, "abs_a00": 2048, "abs_a01": 3072, "a_kept00": 4096}
+
+        def held(name, shape, dtype):
+            if name in places:
+                return shared.tile(shape, dtype, name=name, offset=places[name], align_bytes=64)
+            return sbuf(name, shape, dtype)
 
         def new_bank():
             return psum.tile([P, PACK, CHUNK], F32, name="bank")
@@ -48,45 +56,44 @@ def tile_list_lens_pair_balance_kernel(
         nc.gpsimd.memset(w2_plane_raw[:].bitcast(I32), 0)
         warm_in = sbuf("warm_in", [P, 8], F32)
         warm_out = sbuf("warm_out", [P, 8], F32)
-        nc.gpsimd.memset(warm_in[:], 0.0)
+        nc.vector.memset(warm_in[:], 0.0)
         nc.scalar.activation(warm_out[:], warm_in[:], ACT.Gelu_apprx_tanh)
+        for q in range(QUADRANTS):
+            nc.gpsimd.dma_start(
+                w2_plane_raw[32 * q : 32 * q + ROWS, :].bitcast(I32).rearrange("r (a n) -> r a n", a=PASSES),
+                w2_scales[:, ROWS * q : ROWS * (q + 1), :].bitcast(I32).rearrange("a r n -> r a n"),
+            )
 
         tab = [sbuf("tab%d" % a, [P, T], I32) for a in range(PASSES)]
-        w1_raw = {}
 
         def load_tab(a):
             nc.sync.dma_start(tab[a][:], tab_words[a].rearrange("p n i -> p (n i)").bitcast(I32))
 
-        def load_w1(a, b, pieces=1):
-            width = K_PASS // pieces
-            w1_raw[a, b] = []
-            for h in range(pieces):
-                raw = sbuf("w1_raw%d%d%d" % (a, b, h), [P, PACK, width], F32)
-                c0 = K_PASS * b + width * h
-                rows = w1[K_PASS * a : K_PASS * (a + 1), c0 : c0 + width]
-                nc.sync.dma_start(raw[:], rows.rearrange("(p i) c -> p i c", i=PACK))
-                w1_raw[a, b].append(raw)
+        w1_rows = w1.rearrange("(a p i) c -> a p i c", a=PASSES, i=PACK)
+
+        def load_w1(raw, c0):
+            nc.sync.dma_start(raw[:], w1_rows[1, :, :, c0 : c0 + raw.shape[2]])
+            return raw[:]
 
         nc.sync.dma_start(rear_list[:], offs)
         nc.sync.dma_start(front_list[:], offs2)
-        w2_raw = sbuf("w2_raw", [P, PASSES, K // 2], I32)
-        nc.sync.dma_start(w2_raw[:], w2_words.rearrange("a p n -> p a n").bitcast(I32))
+        w1_first = sbuf("w1_first", [P, PACK, K], F32)
+        nc.sync.dma_start(w1_first[:, :1, :], w1_rows[0, :, :1, :])
         for q in range(QUADRANTS):
             nc.sync.dma_start(
                 tab_plane[32 * q : 32 * q + PASSES * ROWS, :].bitcast(I32),
                 tab_scales[:, ROWS * q : ROWS * (q + 1), :].bitcast(I32),
             )
-        load_w1(0, 0)
-        load_w1(1, 0)
-        for q in range(QUADRANTS):
-            nc.sync.dma_start(
-                w2_plane_raw[32 * q : 32 * q + ROWS, :].bitcast(I32).rearrange("r (a n) -> r a n", a=PASSES),
-                w2_scales[:, ROWS * q : ROWS * (q + 1), :].bitcast(I32).rearrange("a r n -> r a n"),
-            )
+        nc.sync.dma_start(w1_first[:, 1:, :], w1_rows[0, :, 1:, :])
+        w1_raw = {(0, b): [w1_first[:, :, K_PASS * b : K_PASS * (b + 1)]] for b in range(PASSES)}
         load_tab(0)
-        load_w1(0, 1)
+        w1_raw[1, 0] = [load_w1(sbuf("w1_raw10", [P, PACK, K_PASS], F32), 0)]
         load_tab(1)
-        load_w1(1, 1, pieces=2)
+        w1_raw110 = shared.tile([P, PACK, K_PASS // 2], F32, name="w1_raw110", offset=1024, align_bytes=64)
+        w1_raw111 = sbuf("w1_raw111", [P, PACK, K_PASS // 2], F32)
+        w1_raw[1, 1] = [load_w1(w1_raw110, K_PASS), load_w1(w1_raw111, K_PASS + K_PASS // 2)]
+        w2_raw = sbuf("w2_raw", [P, PASSES, K // 2], I32)
+        nc.sync.dma_start(w2_raw[:], w2_words.rearrange("a p n -> p a n").bitcast(I32))
         prior_sb = []
         for g in range(2):
             prior_sb.append(sbuf("prior%d" % g, [P, PACK, S], F32))
@@ -113,18 +120,13 @@ def tile_list_lens_pair_balance_kernel(
                 )
             return codes, plane
 
-        def quantize_w1(a, b, vector_share, piece):
+        def quantize_w1(a, b, on_vector, piece):
             dealt = sbuf("w1_dealt%d%d" % (a, b), [P, PACK * K_PASS], BF16)
             dst = dealt[:].rearrange("p (t m i) -> p m i t", t=PACK, i=PACK)
-            m0 = 0
-            for raw in w1_raw[a, b]:
-                src = raw[:].rearrange("p i (m t) -> p m i t", t=PACK)
-                count = src.shape[1]
-                split = count - (vector_share if raw is w1_raw[a, b][-1] else 0)
-                nc.scalar.copy(dst[:, m0 : m0 + split], src[:, :split])
-                if split < count:
-                    nc.vector.tensor_copy(dst[:, m0 + split : m0 + count], src[:, split:])
-                m0 = m0 + count
+            copy = nc.vector.tensor_copy if on_vector else nc.scalar.copy
+            count = P // len(w1_raw[a, b])
+            for h, raw in enumerate(w1_raw[a, b]):
+                copy(dst[:, count * h : count * (h + 1)], raw.rearrange("p i (m t) -> p m i t", t=PACK))
             return quantize("w1_%d%d" % (a, b), dealt, K_PASS, piece)
 
         def mx_pass(bank, a, stationary, moving):
@@ -147,8 +149,7 @@ def tile_list_lens_pair_balance_kernel(
 
         rear_plane = gather("rear_plane", tab_plane[:], rear_list, S, U8, S)
         w1_q = {}
-        w1_q[0, 0] = quantize_w1(0, 0, 0, K_PASS)
-        w1_q[1, 0] = quantize_w1(1, 0, 0, K_PASS)
+        w1_q[0, 0] = quantize_w1(0, 0, False, K_PASS)
         rear = [gather("rear0", tab[0][:].bitcast(U32), rear_list, S, U32, S)]
         a_bank = {}
 
@@ -164,46 +165,54 @@ def tile_list_lens_pair_balance_kernel(
         for c in range(CHUNKS):
             a_bank[0, c] = new_bank()
             stage1_pass(0, 0, c)
-        w1_q[0, 1] = quantize_w1(0, 1, 0, K_PASS)
+        w1_q[0, 1] = quantize_w1(0, 1, False, K_PASS)
         for c in range(CHUNKS):
             a_bank[1, c] = new_bank()
             stage1_pass(0, 1, c)
+        w1_q[1, 0] = quantize_w1(1, 0, False, K_PASS)
         rear.append(gather("rear1", tab[1][:].bitcast(U32), rear_list, S, U32, S // 2))
-        w1_q[1, 1] = quantize_w1(1, 1, 32, 2 * P)
+        w1_q[1, 1] = quantize_w1(1, 1, False, 2 * P)
 
         w2_codes = sbuf("w2_codes", [P, PASSES * 2 * K], U8)
-        w2_plane = sbuf("w2_plane", [P, PASSES * K], U8)
+        w2_plane = sbuf("w2_plane", [P, PASSES * K], U8, "w1_dealt10")
 
         def deal_w2():
             nc.vector.tensor_copy(
                 w2_plane[:].rearrange("p (g t m) -> p g t m", t=PACK, m=P),
                 w2_plane_raw[:].rearrange("p (g m t) -> p g t m", t=PACK, m=P),
             )
-            for a in range(PASSES):
-                nc.vector.tensor_copy(
-                    w2_codes[:, 2 * K * a : 2 * K * (a + 1)].bitcast(U16).rearrange("p (b t m) -> p b t m", t=PACK, m=P),
-                    w2_raw[:, a, :].bitcast(U16).rearrange("p (b m t) -> p b t m", t=PACK, m=P),
-                )
+            nc.vector.tensor_copy(
+                w2_codes[:].bitcast(U16).rearrange("p (g t m) -> p g t m", t=PACK, m=P),
+                w2_raw[:].rearrange("p a n -> p (a n)").bitcast(U16).rearrange("p (g m t) -> p g t m", t=PACK, m=P),
+            )
 
         front = []
         front_plane = []
 
         def gather_front():
             front_plane.append(gather("front_plane", tab_plane[:], front_list, S2, U8, S2))
-            front.append(gather("front0", tab[0][:].bitcast(U32), front_list, S2, U32, S2))
-            front.append(gather("front1", tab[1][:].bitcast(U32), front_list, S2, U32, S, tag="w1_dealt11"))
+            both = gather("front0", tab[0][:].bitcast(U32), front_list, S2, U32, S2)
+            front.append([both[:, :S], both[:, S:]])
+            halves = []
+            for g in range(2):
+                picked = sbuf("front1%d" % g, [P, S], U32, "w1_dealt11" if g else None)
+                nc.vector.tensor_copy(
+                    picked[:], tab[1][:].bitcast(U32).indirect(front_list[:, S // 16 * g : S // 16 * (g + 1)])
+                )
+                halves.append(picked[:])
+            front.append(halves)
 
-        for c in range(CHUNKS):
+        def chain_front(c):
             abs_q, a_kept = [], []
             for b in range(PASSES):
                 stage1_pass(1, b, c)
-                abs_a = sbuf("abs_a%d%d" % (b, c), [P, PACK * CHUNK], BF16)
+                abs_a = held("abs_a%d%d" % (b, c), [P, PACK * CHUNK], BF16)
                 nc.scalar.activation(
                     abs_a[:].rearrange("p (j t) -> p j t", t=PACK), interleaved(a_bank[b, c]), ACT.Abs
                 )
                 abs_q.append(quantize("abs_a%d%d" % (b, c), abs_a, CHUNK, CHUNK))
             for b in range(PASSES):
-                a_kept.append(sbuf("a_kept%d%d" % (b, c), [P, CHUNK, PACK], F32))
+                a_kept.append(held("a_kept%d%d" % (b, c), [P, CHUNK, PACK], F32))
                 nc.scalar.copy(a_kept[b][:], interleaved(a_bank[b, c]))
             if c == 0:
                 deal_w2()
@@ -225,9 +234,9 @@ def tile_list_lens_pair_balance_kernel(
                 nc.vector.tensor_tensor(
                     h_values[b][:].rearrange("p (j t) -> p j t", t=PACK), interleaved(b_bank), a_kept[b][:], ALU.max
                 )
-            h_q = [quantize("h%d%d" % (b, c), h_values[b], CHUNK, CHUNK) for b in range(PASSES)]
-            if c == 0:
-                gather_front()
+            return [quantize("h%d%d" % (b, c), h_values[b], CHUNK, CHUNK) for b in range(PASSES)]
+
+        def chain_back(c, h_q):
             for g in range(2):
                 e_bank = new_bank()
                 for a in range(PASSES):
@@ -235,15 +244,24 @@ def tile_list_lens_pair_balance_kernel(
                         e_bank,
                         a,
                         lambda u: (
-                            front[a][:, cols(PACK * g + u)].bitcast(FP8X4),
+                            front[a][g][:, cols(u)].bitcast(FP8X4),
                             front_plane[0][ROWS * a :, cols(PACK * g + u)],
                         ),
                         (h_q[a][0][:].bitcast(FP8X4), h_q[a][1][:]),
                     )
                 x = sbuf("x%d%d" % (g, c), [P, PACK, CHUNK], F32)
-                nc.vector.tensor_tensor(x[:], e_bank[:], prior_sb[g][:, :, cols(c)], ALU.add)
                 y = sbuf("y%d%d" % (g, c), [P, PACK, CHUNK], F32)
-                nc.scalar.activation(y[:], x[:], ACT.Gelu_apprx_tanh)
-                nc.sync.dma_start(
-                    out[K_PASS * g : K_PASS * (g + 1), cols(c)].rearrange("(u p) j -> p u j", p=P), y[:]
-                )
+                rows = out[K_PASS * g : K_PASS * (g + 1), cols(c)].rearrange("(u p) j -> p u j", p=P)
+                step = PACK // 2 if (c, g) == (CHUNKS - 1, 1) else PACK
+                for u0 in range(0, PACK, step):
+                    part = slice(u0, u0 + step)
+                    nc.vector.tensor_tensor(x[:, part], e_bank[:, part], prior_sb[g][:, part, cols(c)], ALU.add)
+                    nc.scalar.activation(y[:, part], x[:, part], ACT.Gelu_apprx_tanh)
+                    nc.sync.dma_start(rows[:, part], y[:, part])
+
+        h_all = [chain_front(0)]
+        gather_front()
+        for c in range(CHUNKS):
+            if c + 1 < CHUNKS:
+                h_all.append(chain_front(c + 1))
+            chain_back(c, h_all[c])

@@ -24,6 +24,7 @@ CHUNK = 128
 CHUNKS = S // CHUNK
 QUADRANTS = 4
 ROWS = 4
+RUN = 4
 
 
 def tile_list_lens_pair_balance_kernel(
@@ -38,7 +39,8 @@ def tile_list_lens_pair_balance_kernel(
         def sbuf(name, shape, dtype, tag=None):
             return keep.tile(shape, dtype, name=name, tag=tag or name, align_bytes=64)
 
-        places = {"a_kept01": 0, "abs_a00": 2048, "abs_a01": 3072, "a_kept00": 4096}
+        places = {"a_kept01": 0, "abs_a00": 2048, "abs_a01": 3072, "a_kept00": 4096,
+                  "a_kept03": 6144, "abs_a02": 8192, "abs_a03": 9216, "a_kept02": 10240}
 
         def held(name, shape, dtype):
             if name in places:
@@ -53,15 +55,16 @@ def tile_list_lens_pair_balance_kernel(
         tab_plane = sbuf("tab_plane", [P, T], U8)
         w2_plane_raw = sbuf("w2_plane_raw", [P, PASSES * K], U8)
         nc.gpsimd.memset(tab_plane[:].bitcast(I32), 0)
-        nc.gpsimd.memset(w2_plane_raw[:].bitcast(I32), 0)
-        warm_in = sbuf("warm_in", [P, 8], F32)
-        warm_out = sbuf("warm_out", [P, 8], F32)
-        nc.vector.memset(warm_in[:], 0.0)
-        nc.scalar.activation(warm_out[:], warm_in[:], ACT.Gelu_apprx_tanh)
-        for q in range(QUADRANTS):
+        nc.vector.memset(w2_plane_raw[:].bitcast(I32), 0)
+        zero = sbuf("zero", [P, 1], F32)
+        no_bias = sbuf("no_bias", [P, 1], F32)
+        nc.gpsimd.memset(zero[:], 0.0)
+        nc.scalar.activation(no_bias[:], zero[:], ACT.Gelu_apprx_tanh)
+
+        for r in range(ROWS):
             nc.gpsimd.dma_start(
-                w2_plane_raw[32 * q : 32 * q + ROWS, :].bitcast(I32).rearrange("r (a n) -> r a n", a=PASSES),
-                w2_scales[:, ROWS * q : ROWS * (q + 1), :].bitcast(I32).rearrange("a r n -> r a n"),
+                w2_plane_raw[r:P:32, :].bitcast(I32).rearrange("q (a n) -> q a n", a=PASSES),
+                w2_scales[:, r::ROWS, :].bitcast(I32).rearrange("a q n -> q a n"),
             )
 
         tab = [sbuf("tab%d" % a, [P, T], I32) for a in range(PASSES)]
@@ -78,19 +81,21 @@ def tile_list_lens_pair_balance_kernel(
         nc.sync.dma_start(rear_list[:], offs)
         nc.sync.dma_start(front_list[:], offs2)
         w1_first = sbuf("w1_first", [P, PACK, K], F32)
-        nc.sync.dma_start(w1_first[:, :1, :], w1_rows[0, :, :1, :])
+        first_flat = w1_first[:].rearrange("p i c -> p (i c)")
+        first_rows = w1_rows[0].rearrange("p i c -> p (i c)")
+        nc.sync.dma_start(first_flat[:, :K_PASS], first_rows[:, :K_PASS])
         for q in range(QUADRANTS):
             nc.sync.dma_start(
                 tab_plane[32 * q : 32 * q + PASSES * ROWS, :].bitcast(I32),
                 tab_scales[:, ROWS * q : ROWS * (q + 1), :].bitcast(I32),
             )
-        nc.sync.dma_start(w1_first[:, 1:, :], w1_rows[0, :, 1:, :])
+        nc.sync.dma_start(first_flat[:, K_PASS:], first_rows[:, K_PASS:])
         w1_raw = {(0, b): [w1_first[:, :, K_PASS * b : K_PASS * (b + 1)]] for b in range(PASSES)}
         load_tab(0)
         w1_raw[1, 0] = [load_w1(sbuf("w1_raw10", [P, PACK, K_PASS], F32), 0)]
         load_tab(1)
         w1_raw110 = shared.tile([P, PACK, K_PASS // 2], F32, name="w1_raw110", offset=1024, align_bytes=64)
-        w1_raw111 = sbuf("w1_raw111", [P, PACK, K_PASS // 2], F32)
+        w1_raw111 = shared.tile([P, PACK, K_PASS // 2], F32, name="w1_raw111", offset=7168, align_bytes=64)
         w1_raw[1, 1] = [load_w1(w1_raw110, K_PASS), load_w1(w1_raw111, K_PASS + K_PASS // 2)]
         w2_raw = sbuf("w2_raw", [P, PASSES, K // 2], I32)
         nc.sync.dma_start(w2_raw[:], w2_words.rearrange("a p n -> p a n").bitcast(I32))
@@ -109,8 +114,8 @@ def tile_list_lens_pair_balance_kernel(
                 )
             return picked
 
-        def quantize(name, values, width, piece):
-            codes = sbuf(name + "_codes", [P, width], U32)
+        def quantize(name, values, width, piece, tag=None):
+            codes = sbuf(name + "_codes", [P, width], U32, tag)
             plane = sbuf(name + "_plane", [P, width], U8)
             for c0 in range(0, width, piece):
                 nc.vector.quantize_mx(
@@ -120,14 +125,14 @@ def tile_list_lens_pair_balance_kernel(
                 )
             return codes, plane
 
-        def quantize_w1(a, b, on_vector, piece):
+        def quantize_w1(a, b, on_vector, piece, tag=None):
             dealt = sbuf("w1_dealt%d%d" % (a, b), [P, PACK * K_PASS], BF16)
             dst = dealt[:].rearrange("p (t m i) -> p m i t", t=PACK, i=PACK)
             copy = nc.vector.tensor_copy if on_vector else nc.scalar.copy
             count = P // len(w1_raw[a, b])
             for h, raw in enumerate(w1_raw[a, b]):
                 copy(dst[:, count * h : count * (h + 1)], raw.rearrange("p i (m t) -> p m i t", t=PACK))
-            return quantize("w1_%d%d" % (a, b), dealt, K_PASS, piece)
+            return quantize("w1_%d%d" % (a, b), dealt, K_PASS, piece, tag)
 
         def mx_pass(bank, a, stationary, moving):
             for t in range(PACK):
@@ -142,12 +147,16 @@ def tile_list_lens_pair_balance_kernel(
                 )
 
         def interleaved(bank):
-            return bank[:].rearrange("p t j -> p j t")
+            return bank[:].rearrange("p t (w i) -> p w t i", i=RUN)
+
+        def woven(values):
+            return values[:].rearrange("p (w i t) -> p w t i", i=RUN, t=PACK)
 
         def cols(i):
             return slice(P * i, P * (i + 1))
 
         rear_plane = gather("rear_plane", tab_plane[:], rear_list, S, U8, S)
+        front_plane = gather("front_plane", tab_plane[:], front_list, S2, U8, S2)
         w1_q = {}
         w1_q[0, 0] = quantize_w1(0, 0, False, K_PASS)
         rear = [gather("rear0", tab[0][:].bitcast(U32), rear_list, S, U32, S)]
@@ -165,7 +174,8 @@ def tile_list_lens_pair_balance_kernel(
         for c in range(CHUNKS):
             a_bank[0, c] = new_bank()
             stage1_pass(0, 0, c)
-        w1_q[0, 1] = quantize_w1(0, 1, False, K_PASS)
+        front0 = gather("front0", tab[0][:].bitcast(U32), front_list, S2, U32, S2)
+        w1_q[0, 1] = quantize_w1(0, 1, False, K_PASS, "tab0")
         for c in range(CHUNKS):
             a_bank[1, c] = new_bank()
             stage1_pass(0, 1, c)
@@ -173,8 +183,8 @@ def tile_list_lens_pair_balance_kernel(
         rear.append(gather("rear1", tab[1][:].bitcast(U32), rear_list, S, U32, S // 2))
         w1_q[1, 1] = quantize_w1(1, 1, False, 2 * P)
 
-        w2_codes = sbuf("w2_codes", [P, PASSES * 2 * K], U8)
-        w2_plane = sbuf("w2_plane", [P, PASSES * K], U8, "w1_dealt10")
+        w2_codes = sbuf("w2_codes", [P, PASSES * 2 * K], U8, "w1_dealt11")
+        w2_plane = sbuf("w2_plane", [P, PASSES * K], U8, "tab_plane")
 
         def deal_w2():
             nc.vector.tensor_copy(
@@ -187,15 +197,12 @@ def tile_list_lens_pair_balance_kernel(
             )
 
         front = []
-        front_plane = []
 
         def gather_front():
-            front_plane.append(gather("front_plane", tab_plane[:], front_list, S2, U8, S2))
-            both = gather("front0", tab[0][:].bitcast(U32), front_list, S2, U32, S2)
-            front.append([both[:, :S], both[:, S:]])
+            front.append([front0[:, :S], front0[:, S:]])
             halves = []
             for g in range(2):
-                picked = sbuf("front1%d" % g, [P, S], U32, "w1_dealt11" if g else None)
+                picked = sbuf("front1%d" % g, [P, S], U32, "w2_raw" if g else None)
                 nc.vector.tensor_copy(
                     picked[:], tab[1][:].bitcast(U32).indirect(front_list[:, S // 16 * g : S // 16 * (g + 1)])
                 )
@@ -208,11 +215,11 @@ def tile_list_lens_pair_balance_kernel(
                 stage1_pass(1, b, c)
                 abs_a = held("abs_a%d%d" % (b, c), [P, PACK * CHUNK], BF16)
                 nc.scalar.activation(
-                    abs_a[:].rearrange("p (j t) -> p j t", t=PACK), interleaved(a_bank[b, c]), ACT.Abs
+                    woven(abs_a), interleaved(a_bank[b, c]), ACT.Abs
                 )
                 abs_q.append(quantize("abs_a%d%d" % (b, c), abs_a, CHUNK, CHUNK))
             for b in range(PASSES):
-                a_kept.append(held("a_kept%d%d" % (b, c), [P, CHUNK, PACK], F32))
+                a_kept.append(held("a_kept%d%d" % (b, c), [P, CHUNK // RUN, PACK, RUN], F32))
                 nc.scalar.copy(a_kept[b][:], interleaved(a_bank[b, c]))
             if c == 0:
                 deal_w2()
@@ -232,7 +239,7 @@ def tile_list_lens_pair_balance_kernel(
                     )
                 h_values.append(sbuf("h%d%d" % (b, c), [P, PACK * CHUNK], BF16))
                 nc.vector.tensor_tensor(
-                    h_values[b][:].rearrange("p (j t) -> p j t", t=PACK), interleaved(b_bank), a_kept[b][:], ALU.max
+                    woven(h_values[b]), interleaved(b_bank), a_kept[b][:], ALU.max
                 )
             return [quantize("h%d%d" % (b, c), h_values[b], CHUNK, CHUNK) for b in range(PASSES)]
 
@@ -245,7 +252,7 @@ def tile_list_lens_pair_balance_kernel(
                         a,
                         lambda u: (
                             front[a][g][:, cols(u)].bitcast(FP8X4),
-                            front_plane[0][ROWS * a :, cols(PACK * g + u)],
+                            front_plane[ROWS * a :, cols(PACK * g + u)],
                         ),
                         (h_q[a][0][:].bitcast(FP8X4), h_q[a][1][:]),
                     )
@@ -256,7 +263,7 @@ def tile_list_lens_pair_balance_kernel(
                 for u0 in range(0, PACK, step):
                     part = slice(u0, u0 + step)
                     nc.vector.tensor_tensor(x[:, part], e_bank[:, part], prior_sb[g][:, part, cols(c)], ALU.add)
-                    nc.scalar.activation(y[:, part], x[:, part], ACT.Gelu_apprx_tanh)
+                    nc.scalar.activation(y[:, part], x[:, part], ACT.Gelu_apprx_tanh, bias=no_bias[:])
                     nc.sync.dma_start(rows[:, part], y[:, part])
 
         h_all = [chain_front(0)]

from contextlib import ExitStack

import concourse.mybir as mybir

K, T, S, S2 = 1024, 2048, 512, 1024
FLOPS = 2 * K * K * S * 2 + 2 * K * S2 * S

F32 = mybir.dt.float32
BF16 = mybir.dt.bfloat16
I32 = mybir.dt.int32
U32 = mybir.dt.uint32
U16 = mybir.dt.uint16
U8 = mybir.dt.uint8
FP8X4 = mybir.dt.float8_e4m3fn_x4
FP4X4 = mybir.dt.float4_e2m1fn_x4
ACT = mybir.ActivationFunctionType
ALU = mybir.AluOpType

P = 128
PACK = 4
K_PASS = P * PACK
PASSES = K // K_PASS
CHUNK = 128
CHUNKS = S // CHUNK
QUADRANTS = 4
ROWS = 4
RUN = 4


def tile_list_lens_pair_balance_kernel(
    tc, tab_words, tab_scales, offs, offs2, w1, w2_words, w2_scales, prior, out
):
    nc = tc.nc
    with ExitStack() as ctx:
        keep = ctx.enter_context(tc.tile_pool(name="keep", bufs=1))
        shared = ctx.enter_context(tc.tile_pool(name="shared", bufs=1))
        psum = ctx.enter_context(tc.psum_pool(name="psum", bufs=8))

        def sbuf(name, shape, dtype, tag=None):
            return keep.tile(shape, dtype, name=name, tag=tag or name, align_bytes=64)

        places = {"a_kept01": 0, "abs_a00": 2048, "abs_a01": 3072, "a_kept00": 4096,
                  "a_kept03": 6144, "abs_a02": 8192, "abs_a03": 9216, "a_kept02": 10240}

        def held(name, shape, dtype):
            if name in places:
                return shared.tile(shape, dtype, name=name, offset=places[name], align_bytes=64)
            return sbuf(name, shape, dtype)

        def new_bank():
            return psum.tile([P, PACK, CHUNK], F32, name="bank")

        rear_list = sbuf("rear_list", [P, S // 16], U16)
        front_list = sbuf("front_list", [P, S2 // 16], U16)
        tab_plane = sbuf("tab_plane", [P, T], U8)
        w2_plane_raw = sbuf("w2_plane_raw", [P, PASSES * K], U8)
        nc.gpsimd.memset(tab_plane[:].bitcast(I32), 0)
        nc.vector.memset(w2_plane_raw[:].bitcast(I32), 0)
        zero = sbuf("zero", [P, 1], F32)
        no_bias = sbuf("no_bias", [P, 1], F32)
        nc.gpsimd.memset(zero[:], 0.0)
        nc.scalar.activation(no_bias[:], zero[:], ACT.Gelu_apprx_tanh)

        for r in range(ROWS):
            nc.gpsimd.dma_start(
                w2_plane_raw[r:P:32, :].bitcast(I32).rearrange("q (a n) -> q a n", a=PASSES),
                w2_scales[:, r::ROWS, :].bitcast(I32).rearrange("a q n -> q a n"),
            )

        tab = [sbuf("tab%d" % a, [P, T], I32) for a in range(PASSES)]

        def load_tab(a):
            nc.sync.dma_start(tab[a][:], tab_words[a].rearrange("p n i -> p (n i)").bitcast(I32))

        w1_rows = w1.rearrange("(a p i) c -> a p i c", a=PASSES, i=PACK)

        def load_w1(raw, c0):
            nc.sync.dma_start(raw[:], w1_rows[1, :, :, c0 : c0 + raw.shape[2]])
            return raw[:]

        nc.sync.dma_start(rear_list[:], offs)
        nc.sync.dma_start(front_list[:], offs2)
        w1_first = sbuf("w1_first", [P, PACK, K], F32)
        first_flat = w1_first[:].rearrange("p i c -> p (i c)")
        first_rows = w1_rows[0].rearrange("p i c -> p (i c)")
        nc.sync.dma_start(first_flat[:, :K_PASS], first_rows[:, :K_PASS])
        for q in range(QUADRANTS):
            nc.sync.dma_start(
                tab_plane[32 * q : 32 * q + PASSES * ROWS, :].bitcast(I32),
                tab_scales[:, ROWS * q : ROWS * (q + 1), :].bitcast(I32),
            )
        nc.sync.dma_start(first_flat[:, K_PASS:], first_rows[:, K_PASS:])
        w1_raw = {(0, b): [w1_first[:, :, K_PASS * b : K_PASS * (b + 1)]] for b in range(PASSES)}
        load_tab(0)
        w1_raw[1, 0] = [load_w1(sbuf("w1_raw10", [P, PACK, K_PASS], F32), 0)]
        load_tab(1)
        w1_raw110 = shared.tile([P, PACK, K_PASS // 2], F32, name="w1_raw110", offset=1024, align_bytes=64)
        w1_raw111 = shared.tile([P, PACK, K_PASS // 2], F32, name="w1_raw111", offset=7168, align_bytes=64)
        w1_raw[1, 1] = [load_w1(w1_raw110, K_PASS), load_w1(w1_raw111, K_PASS + K_PASS // 2)]
        w2_raw = sbuf("w2_raw", [P, PASSES, K // 2], I32)
        nc.sync.dma_start(w2_raw[:], w2_words.rearrange("a p n -> p a n").bitcast(I32))
        prior_sb = []
        for g in range(2):
            prior_sb.append(sbuf("prior%d" % g, [P, PACK, S], F32))
            nc.sync.dma_start(
                prior_sb[g][:], prior[K_PASS * g : K_PASS * (g + 1), :].rearrange("(u p) j -> p u j", p=P)
            )

        def gather(name, window, offsets, count, dtype, piece, tag=None):
            picked = sbuf(name, [P, count], dtype, tag)
            for j0 in range(0, count, piece):
                nc.vector.tensor_copy(
                    picked[:, j0 : j0 + piece], window.indirect(offsets[:, j0 // 16 : (j0 + piece) // 16])
                )
            return picked

        def quantize(name, values, width, piece, tag=None):
            codes = sbuf(name + "_codes", [P, width], U32, tag)
            plane = sbuf(name + "_plane", [P, width], U8)
            for c0 in range(0, width, piece):
                nc.vector.quantize_mx(
                    out=codes[:, c0 : c0 + piece].bitcast(FP8X4),
                    scales=plane[:, c0 : c0 + piece],
                    in_=values[:, PACK * c0 : PACK * (c0 + piece)],
                )
            return codes, plane

        def quantize_w1(a, b, on_vector, piece, tag=None):
            dealt = sbuf("w1_dealt%d%d" % (a, b), [P, PACK * K_PASS], BF16)
            dst = dealt[:].rearrange("p (t m i) -> p m i t", t=PACK, i=PACK)
            copy = nc.vector.tensor_copy if on_vector else nc.scalar.copy
            count = P // len(w1_raw[a, b])
            for h, raw in enumerate(w1_raw[a, b]):
                copy(dst[:, count * h : count * (h + 1)], raw.rearrange("p i (m t) -> p m i t", t=PACK))
            return quantize("w1_%d%d" % (a, b), dealt, K_PASS, piece, tag)

        def mx_pass(bank, a, stationary, moving):
            for t in range(PACK):
                nc.tensor.matmul_mx(
                    out=bank[:, t, :],
                    lhsT=stationary(t)[0],
                    lhsT_scale=stationary(t)[1],
                    rhs=moving[0],
                    rhs_scale=moving[1],
                    start=(a == 0 and t == 0),
                    stop=(a == PASSES - 1 and t == PACK - 1),
                )

        def interleaved(bank):
            return bank[:].rearrange("p t (w i) -> p w t i", i=RUN)

        def woven(values):
            return values[:].rearrange("p (w i t) -> p w t i", i=RUN, t=PACK)

        def cols(i):
            return slice(P * i, P * (i + 1))

        rear_plane = gather("rear_plane", tab_plane[:], rear_list, S, U8, S)
        front_plane = gather("front_plane", tab_plane[:], front_list, S2, U8, S2)
        w1_q = {}
        w1_q[0, 0] = quantize_w1(0, 0, False, K_PASS)
        rear = [gather("rear0", tab[0][:].bitcast(U32), rear_list, S, U32, S)]
        a_bank = {}

        def stage1_pass(a, b, c):
            codes, plane = w1_q[a, b]
            mx_pass(
                a_bank[b, c],
                a,
                lambda t: (codes[:, cols(t)].bitcast(FP8X4), plane[:, cols(t)]),
                (rear[a][:, cols(c)].bitcast(FP8X4), rear_plane[ROWS * a :, cols(c)]),
            )

        for c in range(CHUNKS):
            a_bank[0, c] = new_bank()
            stage1_pass(0, 0, c)
        front0 = gather("front0", tab[0][:].bitcast(U32), front_list, S2, U32, S2)
        w1_q[0, 1] = quantize_w1(0, 1, False, K_PASS, "tab0")
        for c in range(CHUNKS):
            a_bank[1, c] = new_bank()
            stage1_pass(0, 1, c)
        w1_q[1, 0] = quantize_w1(1, 0, False, K_PASS)
        rear.append(gather("rear1", tab[1][:].bitcast(U32), rear_list, S, U32, S // 2))
        w1_q[1, 1] = quantize_w1(1, 1, False, 2 * P)

        w2_codes = sbuf("w2_codes", [P, PASSES * 2 * K], U8, "w1_dealt11")
        w2_plane = sbuf("w2_plane", [P, PASSES * K], U8, "tab_plane")

        def deal_w2():
            nc.vector.tensor_copy(
                w2_plane[:].rearrange("p (g t m) -> p g t m", t=PACK, m=P),
                w2_plane_raw[:].rearrange("p (g m t) -> p g t m", t=PACK, m=P),
            )
            nc.vector.tensor_copy(
                w2_codes[:].bitcast(U16).rearrange("p (g t m) -> p g t m", t=PACK, m=P),
                w2_raw[:].rearrange("p a n -> p (a n)").bitcast(U16).rearrange("p (g m t) -> p g t m", t=PACK, m=P),
            )

        front = []

        def gather_front():
            front.append([front0[:, :S], front0[:, S:]])
            halves = []
            for g in range(2):
                picked = sbuf("front1%d" % g, [P, S], U32, "w2_raw" if g else None)
                nc.vector.tensor_copy(
                    picked[:], tab[1][:].bitcast(U32).indirect(front_list[:, S // 16 * g : S // 16 * (g + 1)])
                )
                halves.append(picked[:])
            front.append(halves)

        def chain_front(c):
            abs_q, a_kept = [], []
            for b in range(PASSES):
                stage1_pass(1, b, c)
                abs_a = held("abs_a%d%d" % (b, c), [P, PACK * CHUNK], BF16)
                nc.scalar.activation(
                    woven(abs_a), interleaved(a_bank[b, c]), ACT.Abs
                )
                abs_q.append(quantize("abs_a%d%d" % (b, c), abs_a, CHUNK, CHUNK))
            for b in range(PASSES):
                a_kept.append(held("a_kept%d%d" % (b, c), [P, CHUNK // RUN, PACK, RUN], F32))
                nc.scalar.copy(a_kept[b][:], interleaved(a_bank[b, c]))
            if c == 0:
                deal_w2()
            h_values = []
            for b in range(PASSES):
                b_bank = new_bank()
                for a in range(PASSES):
                    base = K * a + K_PASS * b
                    mx_pass(
                        b_bank,
                        a,
                        lambda t: (
                            w2_codes[:, 2 * (base + P * t) : 2 * (base + P * (t + 1))].bitcast(FP4X4),
                            w2_plane[:, base + P * t : base + P * (t + 1)],
                        ),
                        (abs_q[a][0][:].bitcast(FP8X4), abs_q[a][1][:]),
                    )
                h_values.append(sbuf("h%d%d" % (b, c), [P, PACK * CHUNK], BF16))
                nc.vector.tensor_tensor(
                    woven(h_values[b]), interleaved(b_bank), a_kept[b][:], ALU.max
                )
            return [quantize("h%d%d" % (b, c), h_values[b], CHUNK, CHUNK) for b in range(PASSES)]

        def chain_back(c, h_q):
            for g in range(2):
                e_bank = new_bank()
                for a in range(PASSES):
                    mx_pass(
                        e_bank,
                        a,
                        lambda u: (
                            front[a][g][:, cols(u)].bitcast(FP8X4),
                            front_plane[ROWS * a :, cols(PACK * g + u)],
                        ),
                        (h_q[a][0][:].bitcast(FP8X4), h_q[a][1][:]),
                    )
                x = sbuf("x%d%d" % (g, c), [P, PACK, CHUNK], F32)
                y = sbuf("y%d%d" % (g, c), [P, PACK, CHUNK], F32)
                rows = out[K_PASS * g : K_PASS * (g + 1), cols(c)].rearrange("(u p) j -> p u j", p=P)
                step = PACK // 2 if (c, g) == (CHUNKS - 1, 1) else PACK
                for u0 in range(0, PACK, step):
                    part = slice(u0, u0 + step)
                    nc.vector.tensor_tensor(x[:, part], e_bank[:, part], prior_sb[g][:, part, cols(c)], ALU.add)
                    nc.scalar.activation(y[:, part], x[:, part], ACT.Gelu_apprx_tanh, bias=no_bias[:])
                    nc.sync.dma_start(rows[:, part], y[:, part])

        h_all = [chain_front(0)]
        gather_front()
        for c in range(CHUNKS):
            if c + 1 < CHUNKS:
                h_all.append(chain_front(c + 1))
            chain_back(c, h_all[c])
